import numpy as np, ml_dtypes
CORES = [9,17,57,81,121,137,145,185,209,249]
N = 10
F = 256
def setup_inputs(rng):
    return {"a": rng.standard_normal((N, 128, 128), dtype=np.float32).astype(ml_dtypes.bfloat16), "w": rng.standard_normal((N, 128, F), dtype=np.float32).astype(ml_dtypes.bfloat16)}
def setup_inputs_big(rng):
    d = setup_inputs(rng)
    for k in ("a", "w"): d[k] = (d[k].astype(np.float32) * 1024.0).astype(d[k].dtype)
    return d
def setup_inputs_small(rng):
    d = setup_inputs(rng)
    for k in ("a", "w"): d[k] = (d[k].astype(np.float32) * (1 / 1024.0)).astype(d[k].dtype)
    return d
def setup_inputs_apart(rng):
    d = setup_inputs(rng)
    f = (10.0 ** rng.permutation(np.linspace(-1.5, 1.5, N))).astype(np.float32).reshape(N, 1, 1)
    for k in ("a", "w"): d[k] = (d[k].astype(np.float32) * f).astype(d[k].dtype)
    return d
def reference(a, w):
    A, W = a.astype(np.float64), w.astype(np.float64)
    p = np.stack([A[j].T @ W[j] for j in range(N)])
    return {"y": np.cumsum(p, axis=0).astype(ml_dtypes.bfloat16 if a.dtype != np.float64 else np.float64)}

@@ -1,0 +1,133 @@
+from concourse.bass import DstId, RemoteDMATransfer
+from concourse.mybir import AluOpType
+
+N, F = 10, 256
+HOSTS = 2
+K_ON = 8
+K_OFF = 8
+SPLIT = 3
+
+SCRATCH = {
+    "a_sb": ("sbuf", [128, 128], "bfloat16"),
+    "w_sb": ("sbuf", [128, F], "bfloat16"),
+    "acc": ("psum", [128, F], "float32"),
+    "p": ("sbuf", [128, F], "bfloat16"),
+    "land": ("sbuf", [128, (N - 1) * F], "bfloat16"),
+    "y_sb": ("sbuf", [128, F], "bfloat16"),
+}
+SEMAPHORES = ["ld", "mm", "vec", "sent", "st"] + ["arr%d" % j for j in range(N - 1)]
+
+
+def _take(mask, k):
+    out, b = 0, 0
+    while k and mask >> b:
+        if (mask >> b) & 1:
+            out |= 1 << b
+            k -= 1
+        b += 1
+    return out
+
+
+def _count(mask):
+    return bin(mask).count("1")
+
+
+def _common(topo, src, dsts):
+    m = topo.mask(src, dsts[0])
+    for d in dsts[1:]:
+        m &= topo.mask(src, d)
+    return m
+
+
+def _plan(T, topo):
+    cores = list(T.cores)
+    world = range(HOSTS * topo.CORES_PER_HOST)
+    plan = {}
+    for j, c in enumerate(cores):
+        later = range(j + 1, len(cores))
+        direct = [r for r in later if topo.may_write(c, cores[r])]
+        cross = [r for r in later if not topo.may_write(c, cores[r])]
+        relays = []
+        if cross:
+            own = [h for h in world if h not in cores and topo.host(h) == topo.host(c) and topo.chip(h) == topo.chip(c)
+                   and all(topo.may_write(h, cores[r]) for r in cross)]
+            near = [h for h in own if topo.die(h) == topo.die(c)]
+            far = [h for h in own if topo.die(h) != topo.die(c)]
+            picks = [near[0], far[0]] if len(cross) >= SPLIT else [far[0]]
+            relays = [(h, cross[i::len(picks)]) for i, h in enumerate(picks)]
+        plan[j] = (relays, direct)
+    return plan
+
+
+def _send(g, T, topo, core, src, j, dsts, mask):
+    ids = []
+    for d in dsts:
+        rid, pid = topo.addr(d, core)
+        ids.append(DstId(rid=rid, pnc=pid))
+    slot = T.land[:, j * F:(j + 1) * F]
+    g.remote_dma_fused([RemoteDMATransfer(dst_ids=ids, dma_engine_mask=mask, remote_sem=T.sem["arr%d" % j],
+                                          srcs=[src], dsts=[slot] * len(ids), alu_op=0)], local_sem=T.sem.sent)
+    return _count(mask)
+
+
+def rank_program(g, core, T, topo):
+    cores = list(T.cores)
+    plan = _plan(T, topo)
+    rank = T.rank_of(core)
+
+    if rank is None:
+        for j in plan:
+            for h, served in plan[j][0]:
+                if h == core:
+                    dsts = [cores[r] for r in served]
+                    g.wait_ge(T.sem["arr%d" % j], K_ON)
+                    n = _send(g, T, topo, core, T.land[:, j * F:(j + 1) * F], j, dsts,
+                              _take(_common(topo, core, dsts), K_OFF))
+                    g.wait_ge(T.sem.sent, n)
+        return
+
+    relays, direct = plan[rank]
+
+    g.sync.dma_start(T.a_sb[:], T.a[:]).then_inc(T.sem.ld, 16)
+    g.scalar.dma_start(T.w_sb[:], T.w[:]).then_inc(T.sem.ld, 16)
+    g.tensor.wait_ge(T.sem.ld, 32)
+    g.tensor.matmul(T.acc[:], T.a_sb[:], T.w_sb[:], True, True).then_inc(T.sem.mm, 1)
+    g.vector.wait_ge(T.sem.mm, 1)
+    done = 0
+    if relays or direct or rank == 0:
+        g.vector.tensor_copy(T.p[:], T.acc[:]).then_inc(T.sem.vec, 1)
+        done = 1
+
+    sent = 0
+    if relays or direct:
+        g.wait_ge(T.sem.vec, 1)
+    off = _take(_common(topo, core, [cores[r] for r in direct]), K_OFF) if direct else 0
+    if relays:
+        hs = [h for h, _ in relays]
+        on = _common(topo, core, hs)
+        sent += _send(g, T, topo, core, T.p[:], rank, hs, _take((on & ~off) or on, K_ON))
+    if direct:
+        sent += _send(g, T, topo, core, T.p[:], rank, [cores[r] for r in direct], off)
+
+    due = []
+    for j in range(rank):
+        rel, dr = plan[j]
+        if rank in dr:
+            due.append((1.0 + dr.index(rank), j))
+        for i, (h, served) in enumerate(rel):
+            if rank in served:
+                due.append((2.5 + (i + 1) + (1 + served.index(rank)), j))
+    due.sort()
+    for k, (_, j) in enumerate(due):
+        g.vector.wait_ge(T.sem["arr%d" % j], K_OFF)
+        if done:
+            g.vector.wait_ge(T.sem.vec, done)
+        out = T.y_sb if k == len(due) - 1 else T.acc
+        g.vector.tensor_tensor(out[:], T.acc[:], T.land[:, j * F:(j + 1) * F], AluOpType.add).then_inc(T.sem.vec, 1)
+        done += 1
+
+    g.sync.wait_ge(T.sem.vec, done)
+    g.sync.dma_start(T.y[:], (T.y_sb if due else T.p)[:]).then_inc(T.sem.st, 16)
+    g.sync.wait_ge(T.sem.st, 16)
+    if sent:
+        g.wait_ge(T.sem.sent, sent)

@@ -5,17 +5,21 @@ N, F = 10, 256
 HOSTS = 2
 K_ON = 8
 K_OFF = 8
-SPLIT = 3
+T_HAND, T_RELAY = 0.7, 8.0
 
 SCRATCH = {
     "a_sb": ("sbuf", [128, 128], "bfloat16"),
     "w_sb": ("sbuf", [128, F], "bfloat16"),
-    "acc": ("psum", [128, F], "float32"),
+    "acc": ("psum", [128, 512], "float32"),
+    "tot": ("psum", [128, 512], "float32"),
     "p": ("sbuf", [128, F], "bfloat16"),
     "land": ("sbuf", [128, (N - 1) * F], "bfloat16"),
     "y_sb": ("sbuf", [128, F], "bfloat16"),
+    "z": ("sbuf", [128, 129], "bfloat16"),
+    "zd": ("dram", [129, 128], "bfloat16"),
+    "ident": ("sbuf", [128, 128], "bfloat16"),
 }
-SEMAPHORES = ["ld", "mm", "vec", "sent", "st"] + ["arr%d" % j for j in range(N - 1)]
+SEMAPHORES = ["ld", "mm", "vec", "sent", "st", "zs", "id1", "id2", "pe"] + ["arr%d" % j for j in range(N - 1)]
 
 
 def _take(mask, k):
@@ -43,19 +47,25 @@ def _plan(T, topo):
     cores = list(T.cores)
     world = range(HOSTS * topo.CORES_PER_HOST)
     plan = {}
+    seen = {}
     for j, c in enumerate(cores):
         later = range(j + 1, len(cores))
         direct = [r for r in later if topo.may_write(c, cores[r])]
         cross = [r for r in later if not topo.may_write(c, cores[r])]
-        relays = []
+        on = []
         if cross:
             own = [h for h in world if h not in cores and topo.host(h) == topo.host(c) and topo.chip(h) == topo.chip(c)
                    and all(topo.may_write(h, cores[r]) for r in cross)]
             near = [h for h in own if topo.die(h) == topo.die(c)]
-            far = [h for h in own if topo.die(h) != topo.die(c)]
-            picks = [near[0], far[0]] if len(cross) >= SPLIT else [far[0]]
-            relays = [(h, cross[i::len(picks)]) for i, h in enumerate(picks)]
-        plan[j] = (relays, direct)
+            other = [h for h in own if topo.die(h) != topo.die(c)]
+            if len(cross) >= 3:
+                picks = [near[0], other[0]]
+            else:
+                twin = seen.get(tuple(cross), 0)
+                seen[tuple(cross)] = twin + 1
+                picks = [near[0]] if twin % 2 else [other[0]]
+            on = [(h, cross[i::len(picks)]) for i, h in enumerate(picks)]
+        plan[j] = (on, direct)
     return plan
 
 
@@ -86,48 +96,68 @@ def rank_program(g, core, T, topo):
                     g.wait_ge(T.sem.sent, n)
         return
 
-    relays, direct = plan[rank]
-
-    g.sync.dma_start(T.a_sb[:], T.a[:]).then_inc(T.sem.ld, 16)
-    g.scalar.dma_start(T.w_sb[:], T.w[:]).then_inc(T.sem.ld, 16)
-    g.tensor.wait_ge(T.sem.ld, 32)
-    g.tensor.matmul(T.acc[:], T.a_sb[:], T.w_sb[:], True, True).then_inc(T.sem.mm, 1)
-    g.vector.wait_ge(T.sem.mm, 1)
-    done = 0
-    if relays or direct or rank == 0:
-        g.vector.tensor_copy(T.p[:], T.acc[:]).then_inc(T.sem.vec, 1)
-        done = 1
-
-    sent = 0
-    if relays or direct:
-        g.wait_ge(T.sem.vec, 1)
-    off = _take(_common(topo, core, [cores[r] for r in direct]), K_OFF) if direct else 0
-    if relays:
-        hs = [h for h, _ in relays]
-        on = _common(topo, core, hs)
-        sent += _send(g, T, topo, core, T.p[:], rank, hs, _take((on & ~off) or on, K_ON))
-    if direct:
-        sent += _send(g, T, topo, core, T.p[:], rank, [cores[r] for r in direct], off)
+    on, direct = plan[rank]
 
     due = []
     for j in range(rank):
-        rel, dr = plan[j]
-        if rank in dr:
-            due.append((1.0 + dr.index(rank), j))
-        for i, (h, served) in enumerate(rel):
+        o, d = plan[j]
+        if rank in d:
+            due.append((1.0 + d.index(rank), j))
+        for i, (h, served) in enumerate(o):
             if rank in served:
-                due.append((2.5 + (i + 1) + (1 + served.index(rank)), j))
-    due.sort()
-    for k, (_, j) in enumerate(due):
-        g.vector.wait_ge(T.sem["arr%d" % j], K_OFF)
+                due.append(((i + 1) * T_HAND + T_RELAY + 1.0 + served.index(rank), j))
+    due = [j for _, j in sorted(due)]
+    early, last = due[:-1], due[-1:]
+
+    g.sync.dma_start(T.a_sb[:], T.a[:]).then_inc(T.sem.ld, 16)
+    g.scalar.dma_start(T.w_sb[:], T.w[:]).then_inc(T.sem.ld, 16)
+    if early:
+        g.vector.memset(T.z[:, 1:129], 0.0).then_inc(T.sem.zs, 1)
+        g.vector.memset(T.z[:, 0:1], 1.0).then_inc(T.sem.zs, 1)
+        g.scalar.wait_ge(T.sem.zs, 2)
+        g.scalar.dma_start(T.zd[:], T.z[:]).then_inc(T.sem.id1, 16)
+        g.scalar.wait_ge(T.sem.id1, 16)
+        g.scalar.dma_start(T.ident[:], T.zd[0:128, :]).then_inc(T.sem.id2, 16)
+
+    g.tensor.wait_ge(T.sem.ld, 32)
+    g.tensor.matmul(T.acc[:, 0:F], T.a_sb[:], T.w_sb[:], True, True).then_inc(T.sem.mm, 1)
+    g.vector.wait_ge(T.sem.mm, 1)
+    done = 0
+    if on or direct or rank == 0:
+        g.vector.tensor_copy(T.p[:], T.acc[:, 0:F]).then_inc(T.sem.vec, 1)
+        done = 1
+    if early:
+        g.tensor.matmul(T.tot[:, 0:F], T.a_sb[:], T.w_sb[:], True, False)
+        g.tensor.wait_ge(T.sem.id2, 16)
+        for k, j in enumerate(early):
+            g.tensor.wait_ge(T.sem["arr%d" % j], K_OFF)
+            mm = g.tensor.matmul(T.tot[:, 0:F], T.ident[:], T.land[:, j * F:(j + 1) * F], False, k == len(early) - 1)
+        mm.then_inc(T.sem.pe, 1)
+
+    sent = 0
+    if on or direct:
+        g.wait_ge(T.sem.vec, 1)
+    off = _take(_common(topo, core, [cores[r] for r in direct]), K_OFF) if direct else 0
+    if on:
+        hs = [h for h, _ in on]
+        m = _common(topo, core, hs)
+        sent += _send(g, T, topo, core, T.p[:], rank, hs, _take((m & ~off) or m, K_ON))
+    if direct:
+        sent += _send(g, T, topo, core, T.p[:], rank, [cores[r] for r in direct], off)
+
+    if last:
+        j = last[0]
+        if early:
+            g.vector.wait_ge(T.sem.pe, 1)
         if done:
             g.vector.wait_ge(T.sem.vec, done)
-        out = T.y_sb if k == len(due) - 1 else T.acc
-        g.vector.tensor_tensor(out[:], T.acc[:], T.land[:, j * F:(j + 1) * F], AluOpType.add).then_inc(T.sem.vec, 1)
+        g.vector.wait_ge(T.sem["arr%d" % j], K_OFF)
+        g.vector.tensor_tensor(T.y_sb[:], (T.tot if early else T.acc)[:, 0:F], T.land[:, j * F:(j + 1) * F],
+                               AluOpType.add).then_inc(T.sem.vec, 1)
         done += 1
 
     g.sync.wait_ge(T.sem.vec, done)
-    g.sync.dma_start(T.y[:], (T.y_sb if due else T.p)[:]).then_inc(T.sem.st, 16)
+    g.sync.dma_start(T.y[:], (T.y_sb if last else T.p)[:]).then_inc(T.sem.st, 16)
     g.sync.wait_ge(T.sem.st, 16)
     if sent:
         g.wait_ge(T.sem.sent, sent)

@@ -1,25 +1,40 @@
 from concourse.bass import DstId, RemoteDMATransfer
-from concourse.mybir import AluOpType
+from concourse.mybir import AluOpType, ActivationFunctionType
 
 N, F = 10, 256
+H = F // 2
 HOSTS = 2
-K_ON = 8
-K_OFF = 8
-T_HAND, T_RELAY = 0.7, 8.0
+K = 8
+T_HAND, T_RELAY, T_DIR, T_FAR = 0.55, 2.0, 0.3, 0.3
+
+RELAYS = {
+    0: [(1, [6, 2]), (0, [3, 8]), (1, [1])],
+    1: [(1, [2, 5]), (0, [4, 7]), (1, [9])],
+    2: [(0, [6, 3]), (0, [5]), (1, [8])],
+    3: [(1, [7, 4]), (1, [6]), (0, [9])],
+    4: [(1, [9, 7]), (0, [8]), (0, [5])],
+    5: [(0, [7, 6]), (0, [9])],
+    6: [(0, [7])],
+    7: [(0, [8])],
+    8: [(0, [9])],
+    9: [],
+}
+DIRECT = {0: [7, 5, 4, 9], 1: [8, 6, 3], 2: [9, 4, 7], 3: [(5, 0), 8], 4: [(6, 0)], 5: [(8, 1)], 6: [(9, 0), 8], 7: [9],
+          8: [], 9: []}
 
 SCRATCH = {
     "a_sb": ("sbuf", [128, 128], "bfloat16"),
     "w_sb": ("sbuf", [128, F], "bfloat16"),
-    "acc": ("psum", [128, 512], "float32"),
+    "acc0": ("psum", [128, 512], "float32"),
+    "acc1": ("psum", [128, 512], "float32"),
     "tot": ("psum", [128, 512], "float32"),
     "p": ("sbuf", [128, F], "bfloat16"),
     "land": ("sbuf", [128, (N - 1) * F], "bfloat16"),
     "y_sb": ("sbuf", [128, F], "bfloat16"),
-    "z": ("sbuf", [128, 129], "bfloat16"),
-    "zd": ("dram", [129, 128], "bfloat16"),
+    "ones": ("sbuf", [128, 128], "bfloat16"),
     "ident": ("sbuf", [128, 128], "bfloat16"),
 }
-SEMAPHORES = ["ld", "mm", "vec", "sent", "st", "zs", "id1", "id2", "pe"] + ["arr%d" % j for j in range(N - 1)]
+SEMAPHORES = ["ld", "mm0", "mm1", "vec", "act", "sent", "st", "zs", "sel", "idr", "pe"] + ["arr%d" % j for j in range(N - 1)]
 
 
 def _take(mask, k):
@@ -32,10 +47,6 @@ def _take(mask, k):
     return out
 
 
-def _count(mask):
-    return bin(mask).count("1")
-
-
 def _common(topo, src, dsts):
     m = topo.mask(src, dsts[0])
     for d in dsts[1:]:
@@ -46,27 +57,38 @@ def _common(topo, src, dsts):
 def _plan(T, topo):
     cores = list(T.cores)
     world = range(HOSTS * topo.CORES_PER_HOST)
-    plan = {}
-    seen = {}
+    fwd, hand, out = {}, {}, {}
+    sup = dict((r, []) for r in range(2, N))
+    spare = []
     for j, c in enumerate(cores):
-        later = range(j + 1, len(cores))
-        direct = [r for r in later if topo.may_write(c, cores[r])]
-        cross = [r for r in later if not topo.may_write(c, cores[r])]
-        on = []
-        if cross:
-            own = [h for h in world if h not in cores and topo.host(h) == topo.host(c) and topo.chip(h) == topo.chip(c)
-                   and all(topo.may_write(h, cores[r]) for r in cross)]
-            near = [h for h in own if topo.die(h) == topo.die(c)]
-            other = [h for h in own if topo.die(h) != topo.die(c)]
-            if len(cross) >= 3:
-                picks = [near[0], other[0]]
+        own = [h for h in world if h not in cores and topo.host(h) == topo.host(c) and topo.chip(h) == topo.chip(c)
+               and all(topo.may_write(h, x) for x in cores)]
+        hand[j] = []
+        for kind, served in RELAYS[j]:
+            h = [x for x in own if (topo.die(x) == topo.die(c)) == bool(kind) and x not in fwd][0]
+            fwd[h] = (j, served)
+            hand[j].append(h)
+            (sup[j] if j in sup else spare).append(h)
+        out[j] = []
+        for e in DIRECT[j]:
+            if e in range(N):
+                out[j].append(cores[e])
             else:
-                twin = seen.get(tuple(cross), 0)
-                seen[tuple(cross)] = twin + 1
-                picks = [near[0]] if twin % 2 else [other[0]]
-            on = [(h, cross[i::len(picks)]) for i, h in enumerate(picks)]
-        plan[j] = (on, direct)
-    return plan
+                r, kind = e
+                h = [x for x in world if topo.mates(x, cores[r]) and topo.may_write(x, cores[r]) and topo.may_write(c, x)
+                     and (topo.die(x) == topo.die(cores[r])) == bool(kind) and x not in fwd][0]
+                fwd[h] = (j, [r])
+                out[j].append(h)
+                sup[r].append(h)
+    few = min(sup, key=lambda r: len(sup[r]))
+    sup[few] = sup[few] + spare
+    return fwd, hand, out, sup
+
+
+def _block(sup, r, core):
+    k, i = len(sup[r]), sup[r].index(core)
+    units = [16 // k + (1 if x < 16 % k else 0) for x in range(k)]
+    return 8 * sum(units[:i]), 8 * sum(units[:i + 1])
 
 
 def _send(g, T, topo, core, src, j, dsts, mask):
@@ -77,86 +99,95 @@ def _send(g, T, topo, core, src, j, dsts, mask):
     slot = T.land[:, j * F:(j + 1) * F]
     g.remote_dma_fused([RemoteDMATransfer(dst_ids=ids, dma_engine_mask=mask, remote_sem=T.sem["arr%d" % j],
                                           srcs=[src], dsts=[slot] * len(ids), alu_op=0)], local_sem=T.sem.sent)
-    return _count(mask)
 
 
 def rank_program(g, core, T, topo):
     cores = list(T.cores)
-    plan = _plan(T, topo)
+    fwd, hand, out, sup = _plan(T, topo)
     rank = T.rank_of(core)
 
     if rank is None:
-        for j in plan:
-            for h, served in plan[j][0]:
-                if h == core:
-                    dsts = [cores[r] for r in served]
-                    g.wait_ge(T.sem["arr%d" % j], K_ON)
-                    n = _send(g, T, topo, core, T.land[:, j * F:(j + 1) * F], j, dsts,
-                              _take(_common(topo, core, dsts), K_OFF))
-                    g.wait_ge(T.sem.sent, n)
+        if core not in fwd:
+            return
+        j, served = fwd[core]
+        dsts = [cores[r] for r in served]
+        mask = _take(_common(topo, core, dsts), K)
+        n = 0
+        for r in sup:
+            if core in sup[r]:
+                c0, c1 = _block(sup, r, core)
+                g.vector.memset(T.ones[:], 1.0).then_inc(T.sem.zs, 1)
+                g.wait_ge(T.sem.zs, 1)
+                g.affine_select(T.ident[:], T.ones[:], [[-1, 128]], AluOpType.is_equal, 0.0, 0, 1).then_inc(T.sem.sel, 1)
+                g.wait_ge(T.sem.sel, 1)
+                rid, pid = topo.addr(cores[r], core)
+                g.remote_dma(T.ident[:, c0:c1], T.ident[:, c0:c1], T.sem.idr, T.sem.sent, pid, rid,
+                             _take(topo.mask(core, cores[r]) & mask, K))
+                n += K
+        g.wait_ge(T.sem["arr%d" % j], K)
+        _send(g, T, topo, core, T.land[:, j * F:(j + 1) * F], j, dsts, mask)
+        g.wait_ge(T.sem.sent, n + K)
         return
-
-    on, direct = plan[rank]
 
     due = []
     for j in range(rank):
-        o, d = plan[j]
-        if rank in d:
-            due.append((1.0 + d.index(rank), j))
-        for i, (h, served) in enumerate(o):
+        for i, e in enumerate(DIRECT[j]):
+            if e == rank:
+                due.append((T_DIR + i + 1.0, j))
+            elif e not in range(N) and e[0] == rank:
+                due.append((T_DIR + i + 1.0 + T_FAR + T_RELAY + 1.0, j))
+        for i, (kind, served) in enumerate(RELAYS[j]):
             if rank in served:
                 due.append(((i + 1) * T_HAND + T_RELAY + 1.0 + served.index(rank), j))
     due = [j for _, j in sorted(due)]
     early, last = due[:-1], due[-1:]
+    sends = bool(hand[rank] or out[rank] or rank == 0)
 
     g.sync.dma_start(T.a_sb[:], T.a[:]).then_inc(T.sem.ld, 16)
     g.scalar.dma_start(T.w_sb[:], T.w[:]).then_inc(T.sem.ld, 16)
-    if early:
-        g.vector.memset(T.z[:, 1:129], 0.0).then_inc(T.sem.zs, 1)
-        g.vector.memset(T.z[:, 0:1], 1.0).then_inc(T.sem.zs, 1)
-        g.scalar.wait_ge(T.sem.zs, 2)
-        g.scalar.dma_start(T.zd[:], T.z[:]).then_inc(T.sem.id1, 16)
-        g.scalar.wait_ge(T.sem.id1, 16)
-        g.scalar.dma_start(T.ident[:], T.zd[0:128, :]).then_inc(T.sem.id2, 16)
 
     g.tensor.wait_ge(T.sem.ld, 32)
-    g.tensor.matmul(T.acc[:, 0:F], T.a_sb[:], T.w_sb[:], True, True).then_inc(T.sem.mm, 1)
-    g.vector.wait_ge(T.sem.mm, 1)
     done = 0
-    if on or direct or rank == 0:
-        g.vector.tensor_copy(T.p[:], T.acc[:, 0:F]).then_inc(T.sem.vec, 1)
+    if sends:
+        g.tensor.matmul(T.acc0[:, 0:H], T.a_sb[:], T.w_sb[:, 0:H], True, True).then_inc(T.sem.mm0, 1)
+        g.tensor.matmul(T.acc1[:, 0:H], T.a_sb[:], T.w_sb[:, H:F], True, True).then_inc(T.sem.mm1, 1)
+        g.vector.wait_ge(T.sem.mm0, 1)
+        g.vector.tensor_copy(T.p[:, 0:H], T.acc0[:, 0:H]).then_inc(T.sem.vec, 1)
+        g.scalar.wait_ge(T.sem.mm1, 1)
+        g.scalar.activation(T.p[:, H:F], T.acc1[:, 0:H], ActivationFunctionType.Copy).then_inc(T.sem.act, 1)
         done = 1
-    if early:
-        g.tensor.matmul(T.tot[:, 0:F], T.a_sb[:], T.w_sb[:], True, False)
-        g.tensor.wait_ge(T.sem.id2, 16)
+    if last:
+        mm = g.tensor.matmul(T.tot[:, 0:F], T.a_sb[:], T.w_sb[:], True, not early)
+        if early:
+            g.tensor.wait_ge(T.sem.idr, K * len(sup[rank]))
         for k, j in enumerate(early):
-            g.tensor.wait_ge(T.sem["arr%d" % j], K_OFF)
+            g.tensor.wait_ge(T.sem["arr%d" % j], K)
             mm = g.tensor.matmul(T.tot[:, 0:F], T.ident[:], T.land[:, j * F:(j + 1) * F], False, k == len(early) - 1)
         mm.then_inc(T.sem.pe, 1)
 
     sent = 0
-    if on or direct:
+    if hand[rank] or out[rank]:
         g.wait_ge(T.sem.vec, 1)
-    off = _take(_common(topo, core, [cores[r] for r in direct]), K_OFF) if direct else 0
-    if on:
-        hs = [h for h, _ in on]
-        m = _common(topo, core, hs)
-        sent += _send(g, T, topo, core, T.p[:], rank, hs, _take((m & ~off) or m, K_ON))
-    if direct:
-        sent += _send(g, T, topo, core, T.p[:], rank, [cores[r] for r in direct], off)
+        g.wait_ge(T.sem.act, 1)
+    off = _take(_common(topo, core, out[rank]), K) if out[rank] else 0
+    if hand[rank]:
+        m = _common(topo, core, hand[rank])
+        _send(g, T, topo, core, T.p[:], rank, hand[rank], _take((m & ~off) or m, K))
+        sent += K
+    if out[rank]:
+        _send(g, T, topo, core, T.p[:], rank, out[rank], off)
+        sent += K
 
     if last:
         j = last[0]
-        if early:
-            g.vector.wait_ge(T.sem.pe, 1)
-        if done:
-            g.vector.wait_ge(T.sem.vec, done)
-        g.vector.wait_ge(T.sem["arr%d" % j], K_OFF)
-        g.vector.tensor_tensor(T.y_sb[:], (T.tot if early else T.acc)[:, 0:F], T.land[:, j * F:(j + 1) * F],
-                               AluOpType.add).then_inc(T.sem.vec, 1)
+        g.vector.wait_ge(T.sem.pe, 1)
+        g.vector.wait_ge(T.sem["arr%d" % j], K)
+        g.vector.tensor_tensor(T.y_sb[:], T.tot[:, 0:F], T.land[:, j * F:(j + 1) * F], AluOpType.add).then_inc(T.sem.vec, 1)
         done += 1
 
     g.sync.wait_ge(T.sem.vec, done)
+    if sends:
+        g.sync.wait_ge(T.sem.act, 1)
     g.sync.dma_start(T.y[:], (T.y_sb if last else T.p)[:]).then_inc(T.sem.st, 16)
     g.sync.wait_ge(T.sem.st, 16)
     if sent:

@@ -33,8 +33,10 @@ SCRATCH = {
     "y_sb": ("sbuf", [128, F], "bfloat16"),
     "ones": ("sbuf", [128, 128], "bfloat16"),
     "ident": ("sbuf", [128, 128], "bfloat16"),
+    "blk": ("sbuf", [128, 128], "bfloat16"),
 }
-SEMAPHORES = ["ld", "mm0", "mm1", "vec", "act", "sent", "st", "zs", "sel", "idr", "pe"] + ["arr%d" % j for j in range(N - 1)]
+SEMAPHORES = (["ld", "mm0", "mm1", "vec", "act", "sent", "st", "zs", "sel", "idr", "pe", "bk"]
+              + ["arr%d" % j for j in range(N - 1)])
 
 
 def _take(mask, k):
@@ -47,6 +49,10 @@ def _take(mask, k):
     return out
 
 
+def _count(mask):
+    return bin(mask).count("1")
+
+
 def _common(topo, src, dsts):
     m = topo.mask(src, dsts[0])
     for d in dsts[1:]:
@@ -57,7 +63,7 @@ def _common(topo, src, dsts):
 def _plan(T, topo):
     cores = list(T.cores)
     world = range(HOSTS * topo.CORES_PER_HOST)
-    fwd, hand, out = {}, {}, {}
+    fwd, hand, out, gift = {}, {}, {}, {}
     sup = dict((r, []) for r in range(2, N))
     spare = []
     for j, c in enumerate(cores):
@@ -68,7 +74,7 @@ def _plan(T, topo):
             h = [x for x in own if (topo.die(x) == topo.die(c)) == bool(kind) and x not in fwd][0]
             fwd[h] = (j, served)
             hand[j].append(h)
-            (sup[j] if j in sup else spare).append(h)
+            (sup[j] if j in sup else spare).append((h, None))
         out[j] = []
         for e in DIRECT[j]:
             if e in range(N):
@@ -79,14 +85,20 @@ def _plan(T, topo):
                      and (topo.die(x) == topo.die(cores[r])) == bool(kind) and x not in fwd][0]
                 fwd[h] = (j, [r])
                 out[j].append(h)
-                sup[r].append(h)
+                sup[r].append((h, None))
     few = min(sup, key=lambda r: len(sup[r]))
     sup[few] = sup[few] + spare
-    return fwd, hand, out, sup
+    for j in range(N):
+        if hand[j]:
+            h = hand[j][-1]
+            t = fwd[h][1][0] if fwd[h][1][0] in sup else min(sup)
+            sup[t].append((h, j))
+            gift[j] = (h, t)
+    return fwd, hand, out, sup, gift
 
 
-def _block(sup, r, core):
-    k, i = len(sup[r]), sup[r].index(core)
+def _block(sup, r, entry):
+    k, i = len(sup[r]), sup[r].index(entry)
     units = [16 // k + (1 if x < 16 % k else 0) for x in range(k)]
     return 8 * sum(units[:i]), 8 * sum(units[:i + 1])
 
@@ -103,7 +115,7 @@ def _send(g, T, topo, core, src, j, dsts, mask):
 
 def rank_program(g, core, T, topo):
     cores = list(T.cores)
-    fwd, hand, out, sup = _plan(T, topo)
+    fwd, hand, out, sup, gift = _plan(T, topo)
     rank = T.rank_of(core)
 
     if rank is None:
@@ -113,17 +125,22 @@ def rank_program(g, core, T, topo):
         dsts = [cores[r] for r in served]
         mask = _take(_common(topo, core, dsts), K)
         n = 0
-        for r in sup:
-            if core in sup[r]:
-                c0, c1 = _block(sup, r, core)
+        todo = [(e[1] is not None, r, e) for r in sorted(sup) for e in sup[r] if e[0] == core]
+        for given, r, e in sorted(todo):
+            c0, c1 = _block(sup, r, e)
+            if given:
+                g.wait_ge(T.sem.bk, _count(topo.mask(cores[e[1]], core)))
+                src = T.blk
+            else:
                 g.vector.memset(T.ones[:], 1.0).then_inc(T.sem.zs, 1)
                 g.wait_ge(T.sem.zs, 1)
                 g.affine_select(T.ident[:], T.ones[:], [[-1, 128]], AluOpType.is_equal, 0.0, 0, 1).then_inc(T.sem.sel, 1)
                 g.wait_ge(T.sem.sel, 1)
-                rid, pid = topo.addr(cores[r], core)
-                g.remote_dma(T.ident[:, c0:c1], T.ident[:, c0:c1], T.sem.idr, T.sem.sent, pid, rid,
-                             _take(topo.mask(core, cores[r]) & mask, K))
-                n += K
+                src = T.ident
+            rid, pid = topo.addr(cores[r], core)
+            g.remote_dma(T.ident[:, c0:c1], src[:, c0:c1], T.sem.idr, T.sem.sent, pid, rid,
+                         _take(topo.mask(core, cores[r]) & mask, K))
+            n += K
         g.wait_ge(T.sem["arr%d" % j], K)
         _send(g, T, topo, core, T.land[:, j * F:(j + 1) * F], j, dsts, mask)
         g.wait_ge(T.sem.sent, n + K)
@@ -146,6 +163,18 @@ def rank_program(g, core, T, topo):
     g.sync.dma_start(T.a_sb[:], T.a[:]).then_inc(T.sem.ld, 16)
     g.scalar.dma_start(T.w_sb[:], T.w[:]).then_inc(T.sem.ld, 16)
 
+    sent = 0
+    if rank in gift:
+        h, t = gift[rank]
+        c0, c1 = _block(sup, t, (h, rank))
+        g.vector.memset(T.ones[:, c0:c1], 1.0).then_inc(T.sem.zs, 1)
+        g.wait_ge(T.sem.zs, 1)
+        g.affine_select(T.blk[:, c0:c1], T.ones[:, c0:c1], [[-1, c1 - c0]], AluOpType.is_equal, 0.0, -c0, 1).then_inc(T.sem.sel, 1)
+        g.wait_ge(T.sem.sel, 1)
+        rid, pid = topo.addr(h, core)
+        g.remote_dma(T.blk[:, c0:c1], T.blk[:, c0:c1], T.sem.bk, T.sem.sent, pid, rid, topo.mask(core, h))
+        sent += _count(topo.mask(core, h))
+
     g.tensor.wait_ge(T.sem.ld, 32)
     done = 0
     if sends:
@@ -165,7 +194,6 @@ def rank_program(g, core, T, topo):
             mm = g.tensor.matmul(T.tot[:, 0:F], T.ident[:], T.land[:, j * F:(j + 1) * F], False, k == len(early) - 1)
         mm.then_inc(T.sem.pe, 1)
 
-    sent = 0
     if hand[rank] or out[rank]:
         g.wait_ge(T.sem.vec, 1)
         g.wait_ge(T.sem.act, 1)

from concourse.bass import DstId, RemoteDMATransfer
from concourse.mybir import AluOpType, ActivationFunctionType

N, F = 10, 256
H = F // 2
HOSTS = 2
K = 8
T_HAND, T_RELAY, T_DIR, T_FAR = 0.55, 2.0, 0.3, 0.3

RELAYS = {
    0: [(1, [6, 2]), (0, [3, 8]), (1, [1])],
    1: [(1, [2, 5]), (0, [4, 7]), (1, [9])],
    2: [(0, [6, 3]), (0, [5]), (1, [8])],
    3: [(1, [7, 4]), (1, [6]), (0, [9])],
    4: [(1, [9, 7]), (0, [8]), (0, [5])],
    5: [(0, [7, 6]), (0, [9])],
    6: [(0, [7])],
    7: [(0, [8])],
    8: [(0, [9])],
    9: [],
}
DIRECT = {0: [7, 5, 4, 9], 1: [8, 6, 3], 2: [9, 4, 7], 3: [(5, 0), 8], 4: [(6, 0)], 5: [(8, 1)], 6: [(9, 0), 8], 7: [9],
          8: [], 9: []}

SCRATCH = {
    "a_sb": ("sbuf", [128, 128], "bfloat16"),
    "w_sb": ("sbuf", [128, F], "bfloat16"),
    "acc0": ("psum", [128, 512], "float32"),
    "acc1": ("psum", [128, 512], "float32"),
    "tot": ("psum", [128, 512], "float32"),
    "p": ("sbuf", [128, F], "bfloat16"),
    "land": ("sbuf", [128, (N - 1) * F], "bfloat16"),
    "y_sb": ("sbuf", [128, F], "bfloat16"),
    "ones": ("sbuf", [128, 128], "bfloat16"),
    "ident": ("sbuf", [128, 128], "bfloat16"),
    "blk": ("sbuf", [128, 128], "bfloat16"),
}
SEMAPHORES = (["ld", "mm0", "mm1", "vec", "act", "sent", "st", "zs", "sel", "idr", "pe", "bk"]
              + ["arr%d" % j for j in range(N - 1)])


def _take(mask, k):
    out, b = 0, 0
    while k and mask >> b:
        if (mask >> b) & 1:
            out |= 1 << b
            k -= 1
        b += 1
    return out


def _count(mask):
    return bin(mask).count("1")


def _common(topo, src, dsts):
    m = topo.mask(src, dsts[0])
    for d in dsts[1:]:
        m &= topo.mask(src, d)
    return m


def _plan(T, topo):
    cores = list(T.cores)
    world = range(HOSTS * topo.CORES_PER_HOST)
    fwd, hand, out, gift = {}, {}, {}, {}
    sup = dict((r, []) for r in range(2, N))
    spare = []
    for j, c in enumerate(cores):
        own = [h for h in world if h not in cores and topo.host(h) == topo.host(c) and topo.chip(h) == topo.chip(c)
               and all(topo.may_write(h, x) for x in cores)]
        hand[j] = []
        for kind, served in RELAYS[j]:
            h = [x for x in own if (topo.die(x) == topo.die(c)) == bool(kind) and x not in fwd][0]
            fwd[h] = (j, served)
            hand[j].append(h)
            (sup[j] if j in sup else spare).append((h, None))
        out[j] = []
        for e in DIRECT[j]:
            if e in range(N):
                out[j].append(cores[e])
            else:
                r, kind = e
                h = [x for x in world if topo.mates(x, cores[r]) and topo.may_write(x, cores[r]) and topo.may_write(c, x)
                     and (topo.die(x) == topo.die(cores[r])) == bool(kind) and x not in fwd][0]
                fwd[h] = (j, [r])
                out[j].append(h)
                sup[r].append((h, None))
    few = min(sup, key=lambda r: len(sup[r]))
    sup[few] = sup[few] + spare
    for j in range(N):
        if hand[j]:
            h = hand[j][-1]
            t = fwd[h][1][0] if fwd[h][1][0] in sup else min(sup)
            sup[t].append((h, j))
            gift[j] = (h, t)
    return fwd, hand, out, sup, gift


def _block(sup, r, entry):
    k, i = len(sup[r]), sup[r].index(entry)
    units = [16 // k + (1 if x < 16 % k else 0) for x in range(k)]
    return 8 * sum(units[:i]), 8 * sum(units[:i + 1])


def _send(g, T, topo, core, src, j, dsts, mask):
    ids = []
    for d in dsts:
        rid, pid = topo.addr(d, core)
        ids.append(DstId(rid=rid, pnc=pid))
    slot = T.land[:, j * F:(j + 1) * F]
    g.remote_dma_fused([RemoteDMATransfer(dst_ids=ids, dma_engine_mask=mask, remote_sem=T.sem["arr%d" % j],
                                          srcs=[src], dsts=[slot] * len(ids), alu_op=0)], local_sem=T.sem.sent)


def rank_program(g, core, T, topo):
    cores = list(T.cores)
    fwd, hand, out, sup, gift = _plan(T, topo)
    rank = T.rank_of(core)

    if rank is None:
        if core not in fwd:
            return
        j, served = fwd[core]
        dsts = [cores[r] for r in served]
        mask = _take(_common(topo, core, dsts), K)
        n = 0
        todo = [(e[1] is not None, r, e) for r in sorted(sup) for e in sup[r] if e[0] == core]
        for given, r, e in sorted(todo):
            c0, c1 = _block(sup, r, e)
            if given:
                g.wait_ge(T.sem.bk, _count(topo.mask(cores[e[1]], core)))
                src = T.blk
            else:
                g.vector.memset(T.ones[:], 1.0).then_inc(T.sem.zs, 1)
                g.wait_ge(T.sem.zs, 1)
                g.affine_select(T.ident[:], T.ones[:], [[-1, 128]], AluOpType.is_equal, 0.0, 0, 1).then_inc(T.sem.sel, 1)
                g.wait_ge(T.sem.sel, 1)
                src = T.ident
            rid, pid = topo.addr(cores[r], core)
            g.remote_dma(T.ident[:, c0:c1], src[:, c0:c1], T.sem.idr, T.sem.sent, pid, rid,
                         _take(topo.mask(core, cores[r]) & mask, K))
            n += K
        g.wait_ge(T.sem["arr%d" % j], K)
        _send(g, T, topo, core, T.land[:, j * F:(j + 1) * F], j, dsts, mask)
        g.wait_ge(T.sem.sent, n + K)
        return

    due = []
    for j in range(rank):
        for i, e in enumerate(DIRECT[j]):
            if e == rank:
                due.append((T_DIR + i + 1.0, j))
            elif e not in range(N) and e[0] == rank:
                due.append((T_DIR + i + 1.0 + T_FAR + T_RELAY + 1.0, j))
        for i, (kind, served) in enumerate(RELAYS[j]):
            if rank in served:
                due.append(((i + 1) * T_HAND + T_RELAY + 1.0 + served.index(rank), j))
    due = [j for _, j in sorted(due)]
    early, last = due[:-1], due[-1:]
    sends = bool(hand[rank] or out[rank] or rank == 0)

    g.sync.dma_start(T.a_sb[:], T.a[:]).then_inc(T.sem.ld, 16)
    g.scalar.dma_start(T.w_sb[:], T.w[:]).then_inc(T.sem.ld, 16)

    sent = 0
    if rank in gift:
        h, t = gift[rank]
        c0, c1 = _block(sup, t, (h, rank))
        g.vector.memset(T.ones[:, c0:c1], 1.0).then_inc(T.sem.zs, 1)
        g.wait_ge(T.sem.zs, 1)
        g.affine_select(T.blk[:, c0:c1], T.ones[:, c0:c1], [[-1, c1 - c0]], AluOpType.is_equal, 0.0, -c0, 1).then_inc(T.sem.sel, 1)
        g.wait_ge(T.sem.sel, 1)
        rid, pid = topo.addr(h, core)
        g.remote_dma(T.blk[:, c0:c1], T.blk[:, c0:c1], T.sem.bk, T.sem.sent, pid, rid, topo.mask(core, h))
        sent += _count(topo.mask(core, h))

    g.tensor.wait_ge(T.sem.ld, 32)
    done = 0
    if sends:
        g.tensor.matmul(T.acc0[:, 0:H], T.a_sb[:], T.w_sb[:, 0:H], True, True).then_inc(T.sem.mm0, 1)
        g.tensor.matmul(T.acc1[:, 0:H], T.a_sb[:], T.w_sb[:, H:F], True, True).then_inc(T.sem.mm1, 1)
        g.vector.wait_ge(T.sem.mm0, 1)
        g.vector.tensor_copy(T.p[:, 0:H], T.acc0[:, 0:H]).then_inc(T.sem.vec, 1)
        g.scalar.wait_ge(T.sem.mm1, 1)
        g.scalar.activation(T.p[:, H:F], T.acc1[:, 0:H], ActivationFunctionType.Copy).then_inc(T.sem.act, 1)
        done = 1
    if last:
        mm = g.tensor.matmul(T.tot[:, 0:F], T.a_sb[:], T.w_sb[:], True, not early)
        if early:
            g.tensor.wait_ge(T.sem.idr, K * len(sup[rank]))
        for k, j in enumerate(early):
            g.tensor.wait_ge(T.sem["arr%d" % j], K)
            mm = g.tensor.matmul(T.tot[:, 0:F], T.ident[:], T.land[:, j * F:(j + 1) * F], False, k == len(early) - 1)
        mm.then_inc(T.sem.pe, 1)

    if hand[rank] or out[rank]:
        g.wait_ge(T.sem.vec, 1)
        g.wait_ge(T.sem.act, 1)
    off = _take(_common(topo, core, out[rank]), K) if out[rank] else 0
    if hand[rank]:
        m = _common(topo, core, hand[rank])
        _send(g, T, topo, core, T.p[:], rank, hand[rank], _take((m & ~off) or m, K))
        sent += K
    if out[rank]:
        _send(g, T, topo, core, T.p[:], rank, out[rank], off)
        sent += K

    if last:
        j = last[0]
        g.vector.wait_ge(T.sem.pe, 1)
        g.vector.wait_ge(T.sem["arr%d" % j], K)
        g.vector.tensor_tensor(T.y_sb[:], T.tot[:, 0:F], T.land[:, j * F:(j + 1) * F], AluOpType.add).then_inc(T.sem.vec, 1)
        done += 1

    g.sync.wait_ge(T.sem.vec, done)
    if sends:
        g.sync.wait_ge(T.sem.act, 1)
    g.sync.dma_start(T.y[:], (T.y_sb if last else T.p)[:]).then_inc(T.sem.st, 16)
    g.sync.wait_ge(T.sem.st, 16)
    if sent:
        g.wait_ge(T.sem.sent, sent)
